import numpy as np
import ml_dtypes


def mxq(x, axis, fmt="e4m3"):
    dtype, down = {"e4m3": (ml_dtypes.float8_e4m3fn, 7), "e5m2": (ml_dtypes.float8_e5m2, 14)}[fmt]
    v = np.moveaxis(np.asarray(x, np.float32).astype(ml_dtypes.bfloat16).astype(np.float64), axis, -1)
    blocks = v.reshape(v.shape[:-1] + (-1, 32))
    amax = np.abs(blocks).max(-1, keepdims=True)
    byte = np.maximum(np.where(amax > 0, np.frexp(amax)[1] - 1 + 127, 0) - down, 1)
    scale = np.exp2(byte - 127.0)
    codes = (blocks / scale).astype(np.float32).astype(dtype).astype(np.float64)
    return np.moveaxis((codes * scale).reshape(v.shape), -1, axis)


WIDE = False


def mx_kscale(k):
    if not WIDE:
        return np.ones(k)
    levels = np.array([10, -10, 5, -5, 0])
    if k % 512:
        return np.exp2(np.random.permutation(np.resize(levels, k // 32))).repeat(32)
    a = np.empty((k // 512, 16))
    for p in range(k // 512):
        a[p, :8] = np.random.permutation(np.resize(levels, 8))
        for g in range(8):
            far = levels[np.abs(levels - a[p, g]) >= 10]
            a[p, g + 8] = far[np.random.randint(len(far))]
    return np.exp2(a.ravel()).repeat(32)


def f64(x):
    return np.asarray(x).astype(np.float64)


def striped8(idx):
    return np.asarray(idx).reshape(8, -1, 16).transpose(0, 2, 1).reshape(128, -1).astype(np.uint16)


def unstriped8(offs):
    return offs.reshape(8, 16, -1).transpose(0, 2, 1).reshape(8, -1).astype(np.int64)


def pick8(x, idx, run):
    r = np.arange(len(x))
    return x[r[:, None], idx[r % (8 * run) // run]]


E2M1 = np.array([0.0, 0.5, 1.0, 1.5, 2.0, 3.0, 4.0, 6.0, -0.0, -0.5, -1.0, -1.5, -2.0, -3.0, -4.0, -6.0])


def pack_weight(w, fmt):
    k, n = w.shape
    w = f64(np.asarray(w, np.float32).astype(ml_dtypes.bfloat16)).reshape(k // 32, 32, n)
    amax = np.abs(w).max(1)
    if fmt == "e4m3":
        byte = np.frexp(amax)[1] - 1 + 127 - 7
    else:
        mant, ex = np.frexp(amax / 6.0)
        byte = np.where(mant > 0.5, ex, ex - 1) + 127
    byte = np.clip(np.where(amax > 0, byte, 1), 1, 254)
    scaled = (w * np.exp2(127.0 - byte)[:, None, :]).reshape(k, n).astype(np.float32)
    by_word = np.ascontiguousarray(scaled.reshape(k // 512, 128, 4, n).transpose(0, 1, 3, 2))
    if fmt == "e4m3":
        words = by_word.astype(ml_dtypes.float8_e4m3fn).view(np.uint8)
    else:
        c = by_word.astype(ml_dtypes.float4_e2m1fn).view(np.uint8) & 0xF
        words = (c[..., 0::2] | (c[..., 1::2] << 4)).reshape(k // 512, 128, 2 * n)
    return np.ascontiguousarray(words), np.ascontiguousarray(byte.astype(np.uint8).reshape(k // 512, 16, n))


def unpack_weight(words, scales, fmt):
    g, _, n = scales.shape
    words = np.ascontiguousarray(words).reshape(g, 128, n, -1)
    if fmt == "e4m3":
        vals = words.view(ml_dtypes.float8_e4m3fn).astype(np.float64)
    else:
        nib = np.empty((g, 128, n, 4), np.uint8)
        nib[..., 0::2] = words & 0xF
        nib[..., 1::2] = words >> 4
        vals = E2M1[nib]
    vals = vals * np.repeat(np.exp2(scales.astype(np.float64) - 127.0), 8, axis=1)[..., None]
    return vals.transpose(0, 1, 3, 2).reshape(g * 512, n)


D, T, U, I, Q = 512, 1024, 1024, 512, 128


def setup_inputs():
    n = np.random.standard_normal
    idx = np.stack([np.random.permutation(T)[:I] for _ in range(8)])
    idx2 = np.stack([np.random.permutation(U)[:I] for _ in range(8)])
    idx3 = np.stack([np.random.permutation(T)[:I] for _ in range(8)])
    idx4 = np.stack([np.random.permutation(U)[:I] for _ in range(8)])
    idx5 = np.stack([np.random.permutation(U)[:I] for _ in range(8)])
    idx6 = np.stack([np.random.permutation(T)[:I] for _ in range(8)])
    fd = mx_kscale(D)
    keysp = pack_weight(n((D, T)) / fd[:, None], "e4m3")
    notesp = pack_weight(n((D, U)) / fd[:, None], "e2m1")
    return {
        "query": (n((D, Q)) * 1.0 / np.sqrt(D) * fd[:, None]).astype(np.float32),
        "keys_words": keysp[0],
        "keys_scales": keysp[1],
        "notes_words": notesp[0],
        "notes_scales": notesp[1],
        "offs": striped8(idx),
        "offs2": striped8(idx2),
        "offs3": striped8(idx3),
        "offs4": striped8(idx4),
        "offs5": striped8(idx5),
        "offs6": striped8(idx6),
    }


def reference(query, keys_words, keys_scales, notes_words, notes_scales, offs, offs2, offs3, offs4, offs5, offs6):
    idx = unstriped8(offs)
    idx2 = unstriped8(offs2)
    idx3 = unstriped8(offs3)
    idx4 = unstriped8(offs4)
    idx5 = unstriped8(offs5)
    idx6 = unstriped8(offs6)
    keysu = unpack_weight(keys_words, keys_scales, "e4m3")
    notesu = unpack_weight(notes_words, notes_scales, "e2m1")
    queryq = mxq(f64(query), 0, "e4m3")
    a = queryq.T @ keysu
    b = queryq.T @ notesu
    f1 = np.zeros((Q, U))
    f1[np.arange(Q)[:, None], idx2[np.arange(Q) % 128 // 16]] = pick8(a, idx, 16)
    f2 = np.zeros((Q, U))
    f2[np.arange(Q)[:, None], idx4[np.arange(Q) % 128 // 16]] = pick8(a, idx3, 16)
    m1 = np.maximum(f1, f2)
    bb = m1 - b
    f3 = np.zeros((Q, T))
    f3[np.arange(Q)[:, None], idx6[np.arange(Q) % 128 // 16]] = pick8(bb, idx5, 16)
    aa = a + f3
    y = pick8(aa, idx, 16)
    return y

@@ -1,0 +1,146 @@
+from contextlib import ExitStack
+
+import concourse.mybir as mybir
+
+D, T, U, I, Q = 512, 1024, 1024, 512, 128
+FLOPS = 2 * D * Q * (T + U)
+
+F32 = mybir.dt.float32
+BF16 = mybir.dt.bfloat16
+I32 = mybir.dt.int32
+U32 = mybir.dt.uint32
+U16 = mybir.dt.uint16
+U8 = mybir.dt.uint8
+FP8X4 = mybir.dt.float8_e4m3fn_x4
+FP4X4 = mybir.dt.float4_e2m1fn_x4
+COPY = mybir.ActivationFunctionType.Copy
+ALU = mybir.AluOpType
+
+P = 128
+PACK = 4
+BANK = 512
+HALF = I // 2
+HALF_COLS = HALF // 16
+A_WIDTHS = (256, 256, 256, 128, 128)
+
+
+def load_scale_rows(engine, plane, rows):
+    for r in range(4):
+        engine.dma_start(out=plane[r:P:32, :].bitcast(I32), in_=rows[r:16:4, :].bitcast(I32))
+
+
+def tile_attend_twowaves_two_kernel(tc, query, keys_words, keys_scales, notes_words, notes_scales,
+                                     offs, offs2, offs3, offs4, offs5, offs6, out):
+    nc = tc.nc
+    with ExitStack() as ctx:
+        lists = ctx.enter_context(tc.tile_pool(name="lists", bufs=1))
+        sb = ctx.enter_context(tc.tile_pool(name="sb", bufs=1))
+        psum = ctx.enter_context(tc.psum_pool(name="psum", bufs=1))
+
+        l1 = lists.tile([P, I // 16], U16, name="l1")
+        l2 = lists.tile([P, I // 16], U16, name="l2")
+        l3 = lists.tile([P, I // 16], U16, name="l3")
+        l4 = lists.tile([P, I // 16], U16, name="l4")
+        l5 = lists.tile([P, I // 16], U16, name="l5")
+        l6 = lists.tile([P, I // 16], U16, name="l6")
+
+        k_plane = sb.tile([P, T], U8, name="k_plane", align_bytes=64)
+        n_plane = sb.tile([P, U], U8, name="n_plane", align_bytes=64)
+        nc.vector.memset(k_plane[:].bitcast(I32), 0)
+
+        q_raw = sb.tile([P, PACK, Q], F32, name="q_raw")
+        nc.sync.dma_start(out=q_raw[:], in_=query.rearrange("(p j) q -> p j q", j=PACK))
+        load_scale_rows(nc.scalar, k_plane, keys_scales[0])
+        k_all = keys_words[0].rearrange("p n t -> p (n t)").bitcast(I32)
+        k_words = []
+        for h in range(2):
+            kw = sb.tile([P, BANK], U32, name="k_words%d" % h, align_bytes=64)
+            nc.sync.dma_start(out=kw[:].bitcast(I32), in_=k_all[:, h * BANK:(h + 1) * BANK])
+            k_words.append(kw)
+        nc.sync.dma_start(l1[:], offs)
+        nc.sync.dma_start(l2[:], offs2)
+        nc.sync.dma_start(l3[:], offs3)
+        nc.sync.dma_start(l4[:], offs4)
+
+        nc.vector.memset(n_plane[:].bitcast(I32), 0)
+        n_words = sb.tile([P, 2 * U], U8, name="n_words", align_bytes=64)
+        nc.sync.dma_start(out=n_words[:].bitcast(I32), in_=notes_words[0].bitcast(I32))
+        load_scale_rows(nc.sync, n_plane, notes_scales[0])
+        nc.sync.dma_start(l5[:], offs5)
+        nc.sync.dma_start(l6[:], offs6)
+
+        f1 = sb.tile([P, U], F32, name="f1")
+        f2 = sb.tile([P, U], F32, name="f2")
+        f3 = sb.tile([P, T], F32, name="f3")
+        nc.vector.memset(f1[:], 0.0)
+        nc.vector.memset(f2[:], 0.0)
+        nc.vector.memset(f3[:], 0.0)
+
+        q_grouped = sb.tile([P, Q, PACK], BF16, name="q_grouped", align_bytes=64)
+        nc.vector.tensor_copy(out=q_grouped[:], in_=q_raw[:].rearrange("p j q -> p q j"))
+        q_codes = sb.tile([P, Q], U32, name="q_codes", align_bytes=64)
+        q_plane = sb.tile([P, Q], U8, name="q_plane", align_bytes=64)
+        nc.vector.quantize_mx(out=q_codes[:].bitcast(FP8X4), scales=q_plane[:],
+                              in_=q_grouped[:].rearrange("p q j -> p (q j)"))
+
+        a = sb.tile([P, T], F32, name="a")
+        c0 = 0
+        a_banks = []
+        for n, width in enumerate(A_WIDTHS):
+            bank = psum.tile([P, width], F32, name="a_bank%d" % n)
+            h, w0 = divmod(c0, BANK)
+            nc.tensor.matmul_mx(out=bank[:], lhsT=q_codes[:].bitcast(FP8X4), lhsT_scale=q_plane[:],
+                                rhs=k_words[h][:, w0:w0 + width].bitcast(FP8X4),
+                                rhs_scale=k_plane[:, c0:c0 + width], start=True, stop=True)
+            if n % 2 == 0:
+                nc.vector.tensor_copy(out=a[:, c0:c0 + width], in_=bank[:])
+            else:
+                nc.scalar.activation(a[:, c0:c0 + width], bank[:], COPY)
+            a_banks.append((bank, c0, width))
+            c0 = c0 + width
+
+        b_banks = []
+        for h in range(2):
+            bank = psum.tile([P, BANK], F32, name="b_bank%d" % h)
+            nc.tensor.matmul_mx(out=bank[:], lhsT=q_codes[:].bitcast(FP8X4), lhsT_scale=q_plane[:],
+                                rhs=n_words[:, 2 * h * BANK:2 * (h + 1) * BANK].bitcast(FP4X4),
+                                rhs_scale=n_plane[:, h * BANK:(h + 1) * BANK], start=True, stop=True)
+            b_banks.append(bank)
+
+        lo, hi = slice(0, HALF_COLS), slice(HALF_COLS, 2 * HALF_COLS)
+        g1a = sb.tile([P, HALF], F32, name="g1a")
+        g1b = sb.tile([P, HALF], F32, name="g1b")
+        g3a = sb.tile([P, HALF], F32, name="g3a")
+        g3b = sb.tile([P, HALF], F32, name="g3b")
+        nc.scalar.activation(g1a[:], a[:].indirect(l1[:, lo]), COPY)
+        nc.vector.tensor_copy(g1b[:], a[:].indirect(l1[:, hi]))
+        nc.scalar.activation(g3a[:], a[:].indirect(l3[:, lo]), COPY)
+        nc.scalar.activation(g3b[:], a[:].indirect(l3[:, hi]), COPY)
+        nc.vector.tensor_copy(f1[:].indirect(l2[:, lo]), g1a[:])
+        nc.vector.tensor_copy(f2[:].indirect(l4[:, lo]), g3a[:])
+        nc.vector.tensor_copy(f1[:].indirect(l2[:, hi]), g1b[:])
+        nc.vector.tensor_copy(f2[:].indirect(l4[:, hi]), g3b[:])
+
+        m1 = sb.tile([P, U], F32, name="m1")
+        bb = sb.tile([P, U], F32, name="bb")
+        for h in range(2):
+            cols = slice(h * BANK, (h + 1) * BANK)
+            nc.vector.tensor_tensor(m1[:, cols], f1[:, cols], f2[:, cols], ALU.max)
+        for h in range(2):
+            cols = slice(h * BANK, (h + 1) * BANK)
+            nc.vector.tensor_tensor(bb[:, cols], m1[:, cols], b_banks[h][:], ALU.subtract)
+
+        g5 = sb.tile([P, I], F32, name="g5")
+        nc.scalar.activation(g5[:, 0:HALF], bb[:].indirect(l5[:, lo]), COPY)
+        nc.vector.tensor_copy(g5[:, HALF:I], bb[:].indirect(l5[:, hi]))
+        nc.vector.tensor_copy(f3[:].indirect(l6[:]), g5[:])
+
+        aa = sb.tile([P, T], F32, name="aa")
+        nc.vector.tensor_tensor(aa[:], a[:], f3[:], ALU.add)
+
+        y0 = sb.tile([P, HALF], F32, name="y0")
+        y1 = sb.tile([P, HALF], F32, name="y1")
+        nc.scalar.activation(y0[:], aa[:].indirect(l1[:, lo]), COPY)
+        nc.vector.tensor_copy(y1[:], aa[:].indirect(l1[:, hi]))
+        nc.scalar.dma_start(out=out[:, 0:HALF], in_=y0[:])
+        nc.sync.dma_start(out=out[:, HALF:I], in_=y1[:])

@@ -19,6 +19,8 @@ ALU = mybir.AluOpType
 P = 128
 PACK = 4
 BANK = 512
+PLANE = 256
+CAST_SPLIT = 80
 HALF = I // 2
 HALF_COLS = HALF // 16
 A_WIDTHS = (256, 256, 256, 128, 128)
@@ -44,25 +46,29 @@ def tile_attend_twowaves_two_kernel(tc, query, keys_words, keys_scales, notes_wo
         l5 = lists.tile([P, I // 16], U16, name="l5")
         l6 = lists.tile([P, I // 16], U16, name="l6")
 
-        k_plane = sb.tile([P, T], U8, name="k_plane", align_bytes=64)
+        k_plane = sb.tile([P, PLANE], U8, name="k_plane", align_bytes=64)
         n_plane = sb.tile([P, U], U8, name="n_plane", align_bytes=64)
         nc.vector.memset(k_plane[:].bitcast(I32), 0)
 
         q_raw = sb.tile([P, PACK, Q], F32, name="q_raw")
         nc.sync.dma_start(out=q_raw[:], in_=query.rearrange("(p j) q -> p j q", j=PACK))
-        load_scale_rows(nc.scalar, k_plane, keys_scales[0])
         k_all = keys_words[0].rearrange("p n t -> p (n t)").bitcast(I32)
         k_words = []
         for h in range(2):
-            kw = sb.tile([P, BANK], U32, name="k_words%d" % h, align_bytes=64)
+            kw = sb.tile([P, BANK], U32, name="k_words%d" % h, tag="k_words%d" % h, align_bytes=64)
             nc.sync.dma_start(out=kw[:].bitcast(I32), in_=k_all[:, h * BANK:(h + 1) * BANK])
             k_words.append(kw)
+            if h == 0:
+                for quad in range(4):
+                    rows = keys_scales[0][4 * quad:4 * quad + 4, :].bitcast(I32)
+                    nc.sync.dma_start(out=k_plane[32 * quad:32 * quad + 16, :].bitcast(I32),
+                                      in_=rows.rearrange("r (h c) -> h r c", h=4))
         nc.sync.dma_start(l1[:], offs)
         nc.sync.dma_start(l2[:], offs2)
         nc.sync.dma_start(l3[:], offs3)
         nc.sync.dma_start(l4[:], offs4)
 
-        nc.vector.memset(n_plane[:].bitcast(I32), 0)
+        nc.gpsimd.memset(n_plane[:].bitcast(I32), 0)
         n_words = sb.tile([P, 2 * U], U8, name="n_words", align_bytes=64)
         nc.sync.dma_start(out=n_words[:].bitcast(I32), in_=notes_words[0].bitcast(I32))
         load_scale_rows(nc.sync, n_plane, notes_scales[0])
@@ -71,17 +77,20 @@ def tile_attend_twowaves_two_kernel(tc, query, keys_words, keys_scales, notes_wo
 
         f1 = sb.tile([P, U], F32, name="f1")
         f2 = sb.tile([P, U], F32, name="f2")
-        f3 = sb.tile([P, T], F32, name="f3")
         nc.vector.memset(f1[:], 0.0)
         nc.vector.memset(f2[:], 0.0)
-        nc.vector.memset(f3[:], 0.0)
 
-        q_grouped = sb.tile([P, Q, PACK], BF16, name="q_grouped", align_bytes=64)
-        nc.vector.tensor_copy(out=q_grouped[:], in_=q_raw[:].rearrange("p j q -> p q j"))
+        q_grouped = sb.tile([P, Q, PACK], BF16, name="q_grouped", tag="q_grouped", align_bytes=64)
+        q_view = q_raw[:].rearrange("p j q -> p q j")
+        nc.vector.tensor_copy(out=q_grouped[:, 0:CAST_SPLIT, :], in_=q_view[:, 0:CAST_SPLIT, :])
+        nc.scalar.activation(q_grouped[:, CAST_SPLIT:Q, :], q_view[:, CAST_SPLIT:Q, :], COPY)
         q_codes = sb.tile([P, Q], U32, name="q_codes", align_bytes=64)
         q_plane = sb.tile([P, Q], U8, name="q_plane", align_bytes=64)
         nc.vector.quantize_mx(out=q_codes[:].bitcast(FP8X4), scales=q_plane[:],
                               in_=q_grouped[:].rearrange("p q j -> p (q j)"))
+
+        f3 = sb.tile([P, T], F32, name="f3", tag="q_grouped", align_bytes=64)
+        nc.vector.memset(f3[:], 0.0)
 
         a = sb.tile([P, T], F32, name="a")
         c0 = 0
@@ -91,8 +100,8 @@ def tile_attend_twowaves_two_kernel(tc, query, keys_words, keys_scales, notes_wo
             h, w0 = divmod(c0, BANK)
             nc.tensor.matmul_mx(out=bank[:], lhsT=q_codes[:].bitcast(FP8X4), lhsT_scale=q_plane[:],
                                 rhs=k_words[h][:, w0:w0 + width].bitcast(FP8X4),
-                                rhs_scale=k_plane[:, c0:c0 + width], start=True, stop=True)
-            if n % 2 == 0:
+                                rhs_scale=k_plane[4 * (c0 // PLANE):P, c0 % PLANE:c0 % PLANE + width], start=True, stop=True)
+            if n in (1, 3, 4):
                 nc.vector.tensor_copy(out=a[:, c0:c0 + width], in_=bank[:])
             else:
                 nc.scalar.activation(a[:, c0:c0 + width], bank[:], COPY)
@@ -108,18 +117,13 @@ def tile_attend_twowaves_two_kernel(tc, query, keys_words, keys_scales, notes_wo
             b_banks.append(bank)
 
         lo, hi = slice(0, HALF_COLS), slice(HALF_COLS, 2 * HALF_COLS)
-        g1a = sb.tile([P, HALF], F32, name="g1a")
-        g1b = sb.tile([P, HALF], F32, name="g1b")
-        g3a = sb.tile([P, HALF], F32, name="g3a")
-        g3b = sb.tile([P, HALF], F32, name="g3b")
-        nc.scalar.activation(g1a[:], a[:].indirect(l1[:, lo]), COPY)
-        nc.vector.tensor_copy(g1b[:], a[:].indirect(l1[:, hi]))
-        nc.scalar.activation(g3a[:], a[:].indirect(l3[:, lo]), COPY)
-        nc.scalar.activation(g3b[:], a[:].indirect(l3[:, hi]), COPY)
-        nc.vector.tensor_copy(f1[:].indirect(l2[:, lo]), g1a[:])
-        nc.vector.tensor_copy(f2[:].indirect(l4[:, lo]), g3a[:])
-        nc.vector.tensor_copy(f1[:].indirect(l2[:, hi]), g1b[:])
-        nc.vector.tensor_copy(f2[:].indirect(l4[:, hi]), g3b[:])
+        g1 = sb.tile([P, I], F32, name="g1")
+        g3 = sb.tile([P, I], F32, name="g3")
+        nc.scalar.activation(g1[:, 0:HALF], a[:].indirect(l1[:, lo]), COPY)
+        nc.vector.tensor_copy(g1[:, HALF:I], a[:].indirect(l1[:, hi]))
+        nc.scalar.activation(g3[:], a[:].indirect(l3[:]), COPY)
+        nc.vector.tensor_copy(f1[:].indirect(l2[:]), g1[:])
+        nc.vector.tensor_copy(f2[:].indirect(l4[:]), g3[:])
 
         m1 = sb.tile([P, U], F32, name="m1")
         bb = sb.tile([P, U], F32, name="bb")

@@ -20,6 +20,7 @@ P = 128
 PACK = 4
 BANK = 512
 PLANE = 256
+SHARE = 704
 CAST_SPLIT = 80
 HALF = I // 2
 HALF_COLS = HALF // 16
@@ -127,12 +128,13 @@ def tile_attend_twowaves_two_kernel(tc, query, keys_words, keys_scales, notes_wo
 
         m1 = sb.tile([P, U], F32, name="m1")
         bb = sb.tile([P, U], F32, name="bb")
-        for h in range(2):
-            cols = slice(h * BANK, (h + 1) * BANK)
+        b_tail = sb.tile([P, U - SHARE], F32, name="b_tail")
+        nc.scalar.activation(b_tail[:], b_banks[1][:, SHARE - BANK:BANK], COPY)
+        for cols in (slice(0, BANK), slice(SHARE, U), slice(BANK, SHARE)):
             nc.vector.tensor_tensor(m1[:, cols], f1[:, cols], f2[:, cols], ALU.max)
-        for h in range(2):
-            cols = slice(h * BANK, (h + 1) * BANK)
-            nc.vector.tensor_tensor(bb[:, cols], m1[:, cols], b_banks[h][:], ALU.subtract)
+        nc.gpsimd.tensor_tensor(bb[:, SHARE:U], m1[:, SHARE:U], b_tail[:], ALU.subtract)
+        nc.vector.tensor_tensor(bb[:, 0:BANK], m1[:, 0:BANK], b_banks[0][:], ALU.subtract)
+        nc.vector.tensor_tensor(bb[:, BANK:SHARE], m1[:, BANK:SHARE], b_banks[1][:, 0:SHARE - BANK], ALU.subtract)
 
         g5 = sb.tile([P, I], F32, name="g5")
         nc.scalar.activation(g5[:, 0:HALF], bb[:].indirect(l5[:, lo]), COPY)
@@ -140,7 +142,11 @@ def tile_attend_twowaves_two_kernel(tc, query, keys_words, keys_scales, notes_wo
         nc.vector.tensor_copy(f3[:].indirect(l6[:]), g5[:])
 
         aa = sb.tile([P, T], F32, name="aa")
-        nc.vector.tensor_tensor(aa[:], a[:], f3[:], ALU.add)
+        nc.gpsimd.tensor_tensor(aa[:, SHARE:T], f3[:, SHARE:T], a[:, SHARE:T], ALU.add)
+        for bank, c0, width in a_banks:
+            c1 = min(c0 + width, SHARE)
+            if c0 < c1:
+                nc.vector.tensor_tensor(aa[:, c0:c1], f3[:, c0:c1], bank[:, 0:c1 - c0], ALU.add)
 
         y0 = sb.tile([P, HALF], F32, name="y0")
         y1 = sb.tile([P, HALF], F32, name="y1")

@@ -19,6 +19,7 @@ ALU = mybir.AluOpType
 P = 128
 PACK = 4
 BANK = 512
+K_LOADS = ((0, 256), (256, 768), (768, 1024))
 PLANE = 256
 SHARE = 704
 CAST_SPLIT = 80
@@ -55,11 +56,11 @@ def tile_attend_twowaves_two_kernel(tc, query, keys_words, keys_scales, notes_wo
         nc.sync.dma_start(out=q_raw[:], in_=query.rearrange("(p j) q -> p j q", j=PACK))
         k_all = keys_words[0].rearrange("p n t -> p (n t)").bitcast(I32)
         k_words = []
-        for h in range(2):
-            kw = sb.tile([P, BANK], U32, name="k_words%d" % h, tag="k_words%d" % h, align_bytes=64)
-            nc.sync.dma_start(out=kw[:].bitcast(I32), in_=k_all[:, h * BANK:(h + 1) * BANK])
+        for n, (c0, c1) in enumerate(K_LOADS):
+            kw = sb.tile([P, c1 - c0], U32, name="k_words%d" % n, align_bytes=64)
+            nc.sync.dma_start(out=kw[:].bitcast(I32), in_=k_all[:, c0:c1])
             k_words.append(kw)
-            if h == 0:
+            if n == 0:
                 for quad in range(4):
                     rows = keys_scales[0][4 * quad:4 * quad + 4, :].bitcast(I32)
                     nc.sync.dma_start(out=k_plane[32 * quad:32 * quad + 16, :].bitcast(I32),
@@ -69,7 +70,7 @@ def tile_attend_twowaves_two_kernel(tc, query, keys_words, keys_scales, notes_wo
         nc.sync.dma_start(l3[:], offs3)
         nc.sync.dma_start(l4[:], offs4)
 
-        nc.gpsimd.memset(n_plane[:].bitcast(I32), 0)
+        nc.vector.memset(n_plane[:].bitcast(I32), 0)
         n_words = sb.tile([P, 2 * U], U8, name="n_words", align_bytes=64)
         nc.sync.dma_start(out=n_words[:].bitcast(I32), in_=notes_words[0].bitcast(I32))
         load_scale_rows(nc.sync, n_plane, notes_scales[0])
@@ -98,7 +99,8 @@ def tile_attend_twowaves_two_kernel(tc, query, keys_words, keys_scales, notes_wo
         a_banks = []
         for n, width in enumerate(A_WIDTHS):
             bank = psum.tile([P, width], F32, name="a_bank%d" % n)
-            h, w0 = divmod(c0, BANK)
+            h = [c0 < end for start, end in K_LOADS].index(True)
+            w0 = c0 - K_LOADS[h][0]
             nc.tensor.matmul_mx(out=bank[:], lhsT=q_codes[:].bitcast(FP8X4), lhsT_scale=q_plane[:],
                                 rhs=k_words[h][:, w0:w0 + width].bitcast(FP8X4),
                                 rhs_scale=k_plane[4 * (c0 // PLANE):P, c0 % PLANE:c0 % PLANE + width], start=True, stop=True)

from contextlib import ExitStack

import concourse.mybir as mybir

D, T, U, I, Q = 512, 1024, 1024, 512, 128
FLOPS = 2 * D * Q * (T + U)

F32 = mybir.dt.float32
BF16 = mybir.dt.bfloat16
I32 = mybir.dt.int32
U32 = mybir.dt.uint32
U16 = mybir.dt.uint16
U8 = mybir.dt.uint8
FP8X4 = mybir.dt.float8_e4m3fn_x4
FP4X4 = mybir.dt.float4_e2m1fn_x4
COPY = mybir.ActivationFunctionType.Copy
ALU = mybir.AluOpType

P = 128
PACK = 4
BANK = 512
K_LOADS = ((0, 256), (256, 768), (768, 1024))
PLANE = 256
SHARE = 704
CAST_SPLIT = 80
HALF = I // 2
HALF_COLS = HALF // 16
A_WIDTHS = (256, 256, 256, 128, 128)


def load_scale_rows(engine, plane, rows):
    for r in range(4):
        engine.dma_start(out=plane[r:P:32, :].bitcast(I32), in_=rows[r:16:4, :].bitcast(I32))


def tile_attend_twowaves_two_kernel(tc, query, keys_words, keys_scales, notes_words, notes_scales,
                                     offs, offs2, offs3, offs4, offs5, offs6, out):
    nc = tc.nc
    with ExitStack() as ctx:
        lists = ctx.enter_context(tc.tile_pool(name="lists", bufs=1))
        sb = ctx.enter_context(tc.tile_pool(name="sb", bufs=1))
        psum = ctx.enter_context(tc.psum_pool(name="psum", bufs=1))

        l1 = lists.tile([P, I // 16], U16, name="l1")
        l2 = lists.tile([P, I // 16], U16, name="l2")
        l3 = lists.tile([P, I // 16], U16, name="l3")
        l4 = lists.tile([P, I // 16], U16, name="l4")
        l5 = lists.tile([P, I // 16], U16, name="l5")
        l6 = lists.tile([P, I // 16], U16, name="l6")

        k_plane = sb.tile([P, PLANE], U8, name="k_plane", align_bytes=64)
        n_plane = sb.tile([P, U], U8, name="n_plane", align_bytes=64)
        nc.vector.memset(k_plane[:].bitcast(I32), 0)

        q_raw = sb.tile([P, PACK, Q], F32, name="q_raw")
        nc.sync.dma_start(out=q_raw[:], in_=query.rearrange("(p j) q -> p j q", j=PACK))
        k_all = keys_words[0].rearrange("p n t -> p (n t)").bitcast(I32)
        k_words = []
        for n, (c0, c1) in enumerate(K_LOADS):
            kw = sb.tile([P, c1 - c0], U32, name="k_words%d" % n, align_bytes=64)
            nc.sync.dma_start(out=kw[:].bitcast(I32), in_=k_all[:, c0:c1])
            k_words.append(kw)
            if n == 0:
                for quad in range(4):
                    rows = keys_scales[0][4 * quad:4 * quad + 4, :].bitcast(I32)
                    nc.sync.dma_start(out=k_plane[32 * quad:32 * quad + 16, :].bitcast(I32),
                                      in_=rows.rearrange("r (h c) -> h r c", h=4))
        nc.sync.dma_start(l1[:], offs)
        nc.sync.dma_start(l2[:], offs2)
        nc.sync.dma_start(l3[:], offs3)
        nc.sync.dma_start(l4[:], offs4)

        nc.vector.memset(n_plane[:].bitcast(I32), 0)
        n_words = sb.tile([P, 2 * U], U8, name="n_words", align_bytes=64)
        nc.sync.dma_start(out=n_words[:].bitcast(I32), in_=notes_words[0].bitcast(I32))
        load_scale_rows(nc.sync, n_plane, notes_scales[0])
        nc.sync.dma_start(l5[:], offs5)
        nc.sync.dma_start(l6[:], offs6)

        f1 = sb.tile([P, U], F32, name="f1")
        f2 = sb.tile([P, U], F32, name="f2")
        nc.vector.memset(f1[:], 0.0)
        nc.vector.memset(f2[:], 0.0)

        q_grouped = sb.tile([P, Q, PACK], BF16, name="q_grouped", tag="q_grouped", align_bytes=64)
        q_view = q_raw[:].rearrange("p j q -> p q j")
        nc.vector.tensor_copy(out=q_grouped[:, 0:CAST_SPLIT, :], in_=q_view[:, 0:CAST_SPLIT, :])
        nc.scalar.activation(q_grouped[:, CAST_SPLIT:Q, :], q_view[:, CAST_SPLIT:Q, :], COPY)
        q_codes = sb.tile([P, Q], U32, name="q_codes", align_bytes=64)
        q_plane = sb.tile([P, Q], U8, name="q_plane", align_bytes=64)
        nc.vector.quantize_mx(out=q_codes[:].bitcast(FP8X4), scales=q_plane[:],
                              in_=q_grouped[:].rearrange("p q j -> p (q j)"))

        f3 = sb.tile([P, T], F32, name="f3", tag="q_grouped", align_bytes=64)
        nc.vector.memset(f3[:], 0.0)

        a = sb.tile([P, T], F32, name="a")
        c0 = 0
        a_banks = []
        for n, width in enumerate(A_WIDTHS):
            bank = psum.tile([P, width], F32, name="a_bank%d" % n)
            h = [c0 < end for start, end in K_LOADS].index(True)
            w0 = c0 - K_LOADS[h][0]
            nc.tensor.matmul_mx(out=bank[:], lhsT=q_codes[:].bitcast(FP8X4), lhsT_scale=q_plane[:],
                                rhs=k_words[h][:, w0:w0 + width].bitcast(FP8X4),
                                rhs_scale=k_plane[4 * (c0 // PLANE):P, c0 % PLANE:c0 % PLANE + width], start=True, stop=True)
            if n in (1, 3, 4):
                nc.vector.tensor_copy(out=a[:, c0:c0 + width], in_=bank[:])
            else:
                nc.scalar.activation(a[:, c0:c0 + width], bank[:], COPY)
            a_banks.append((bank, c0, width))
            c0 = c0 + width

        b_banks = []
        for h in range(2):
            bank = psum.tile([P, BANK], F32, name="b_bank%d" % h)
            nc.tensor.matmul_mx(out=bank[:], lhsT=q_codes[:].bitcast(FP8X4), lhsT_scale=q_plane[:],
                                rhs=n_words[:, 2 * h * BANK:2 * (h + 1) * BANK].bitcast(FP4X4),
                                rhs_scale=n_plane[:, h * BANK:(h + 1) * BANK], start=True, stop=True)
            b_banks.append(bank)

        lo, hi = slice(0, HALF_COLS), slice(HALF_COLS, 2 * HALF_COLS)
        g1 = sb.tile([P, I], F32, name="g1")
        g3 = sb.tile([P, I], F32, name="g3")
        nc.scalar.activation(g1[:, 0:HALF], a[:].indirect(l1[:, lo]), COPY)
        nc.vector.tensor_copy(g1[:, HALF:I], a[:].indirect(l1[:, hi]))
        nc.scalar.activation(g3[:], a[:].indirect(l3[:]), COPY)
        nc.vector.tensor_copy(f1[:].indirect(l2[:]), g1[:])
        nc.vector.tensor_copy(f2[:].indirect(l4[:]), g3[:])

        m1 = sb.tile([P, U], F32, name="m1")
        bb = sb.tile([P, U], F32, name="bb")
        b_tail = sb.tile([P, U - SHARE], F32, name="b_tail")
        nc.scalar.activation(b_tail[:], b_banks[1][:, SHARE - BANK:BANK], COPY)
        for cols in (slice(0, BANK), slice(SHARE, U), slice(BANK, SHARE)):
            nc.vector.tensor_tensor(m1[:, cols], f1[:, cols], f2[:, cols], ALU.max)
        nc.gpsimd.tensor_tensor(bb[:, SHARE:U], m1[:, SHARE:U], b_tail[:], ALU.subtract)
        nc.vector.tensor_tensor(bb[:, 0:BANK], m1[:, 0:BANK], b_banks[0][:], ALU.subtract)
        nc.vector.tensor_tensor(bb[:, BANK:SHARE], m1[:, BANK:SHARE], b_banks[1][:, 0:SHARE - BANK], ALU.subtract)

        g5 = sb.tile([P, I], F32, name="g5")
        nc.scalar.activation(g5[:, 0:HALF], bb[:].indirect(l5[:, lo]), COPY)
        nc.vector.tensor_copy(g5[:, HALF:I], bb[:].indirect(l5[:, hi]))
        nc.vector.tensor_copy(f3[:].indirect(l6[:]), g5[:])

        aa = sb.tile([P, T], F32, name="aa")
        nc.gpsimd.tensor_tensor(aa[:, SHARE:T], f3[:, SHARE:T], a[:, SHARE:T], ALU.add)
        for bank, c0, width in a_banks:
            c1 = min(c0 + width, SHARE)
            if c0 < c1:
                nc.vector.tensor_tensor(aa[:, c0:c1], f3[:, c0:c1], bank[:, 0:c1 - c0], ALU.add)

        y0 = sb.tile([P, HALF], F32, name="y0")
        y1 = sb.tile([P, HALF], F32, name="y1")
        nc.scalar.activation(y0[:], aa[:].indirect(l1[:, lo]), COPY)
        nc.vector.tensor_copy(y1[:], aa[:].indirect(l1[:, hi]))
        nc.scalar.dma_start(out=out[:, 0:HALF], in_=y0[:])
        nc.sync.dma_start(out=out[:, HALF:I], in_=y1[:])
